import numpy as np
import ml_dtypes


def mxq(x, axis, fmt="e4m3"):
    dtype, down = {"e4m3": (ml_dtypes.float8_e4m3fn, 7), "e5m2": (ml_dtypes.float8_e5m2, 14)}[fmt]
    v = np.moveaxis(np.asarray(x, np.float32).astype(ml_dtypes.bfloat16).astype(np.float64), axis, -1)
    blocks = v.reshape(v.shape[:-1] + (-1, 32))
    amax = np.abs(blocks).max(-1, keepdims=True)
    byte = np.maximum(np.where(amax > 0, np.frexp(amax)[1] - 1 + 127, 0) - down, 1)
    scale = np.exp2(byte - 127.0)
    codes = (blocks / scale).astype(np.float32).astype(dtype).astype(np.float64)
    return np.moveaxis((codes * scale).reshape(v.shape), -1, axis)


WIDE = False


def mx_kscale(k):
    if not WIDE:
        return np.ones(k)
    levels = np.array([30, -30])
    if k % 512:
        return np.exp2(np.random.permutation(np.resize(levels, k // 32))).repeat(32)
    a = np.empty((k // 512, 16))
    for p in range(k // 512):
        a[p, :8] = np.random.permutation(np.resize(levels, 8))
        for g in range(8):
            far = levels[np.abs(levels - a[p, g]) >= 10]
            a[p, g + 8] = far[np.random.randint(len(far))]
    return np.exp2(a.ravel()).repeat(32)


def f64(x):
    return np.asarray(x).astype(np.float64)


K, L, M, T = 2048, 1024, 1024, 1024


def setup_inputs():
    n = np.random.standard_normal
    s1 = mx_kscale(K)[:, None]
    s2 = mx_kscale(L)[:, None]
    m = np.exp(0.5 * n((1, T)))
    return {
        "w": (n((K, M)) / np.sqrt(K) / s1).astype(np.float32),
        "dy": (m * n((K, T)) * s1).astype(np.float32),
        "v": (n((L, M)) / np.sqrt(L) / s2).astype(np.float32),
        "e": (n((L, T)) * s2).astype(np.float32),
        "g": (n((1024, 1024))).astype(np.float32),
    }


def reference(w, dy, v, e, g):
    w_ = mxq(f64(w), 0, "e4m3")
    dy_ = mxq(f64(dy), 0, "e5m2")
    v_ = mxq(f64(v), 0, "e4m3")
    e_ = mxq(f64(e), 0, "e4m3")
    y = w_.T @ dy_ + v_.T @ e_
    return f64(g) * y

@@ -1,0 +1,206 @@
+from contextlib import ExitStack
+
+import concourse.mybir as mybir
+
+K, L, D, T = 2048, 1024, 1024, 1024
+FLOPS = 2 * D * T * (K + L)
+
+F32 = mybir.dt.float32
+BF16 = mybir.dt.bfloat16
+U32 = mybir.dt.uint32
+U8 = mybir.dt.uint8
+E4M3 = mybir.dt.float8_e4m3fn_x4
+E5M2 = mybir.dt.float8_e5m2_x4
+
+P = 128
+PACK = 4
+ROWS = P * PACK
+HALF = 512
+TILES = HALF // P
+PASSES = (K + L) // ROWS
+PERM = True
+RAW_BUFS = 5
+V_COLS = 640
+
+
+def tile_mix_aux_fm_mul_kernel(tc, w, dy, v, e, g, out):
+    nc = tc.nc
+    with ExitStack() as ctx:
+        raws = ctx.enter_context(tc.tile_pool(name="raws", bufs=RAW_BUFS))
+        groups = ctx.enter_context(tc.tile_pool(name="groups", bufs=3))
+        keep = ctx.enter_context(tc.tile_pool(name="keep", bufs=1))
+        psum = ctx.enter_context(tc.psum_pool(name="psum", bufs=1))
+        ctx.enter_context(tc.manual_schedule())
+
+        codes = {}
+        scales = {}
+        for side in ("stat", "mov"):
+            codes[side] = keep.tile([P, PASSES, D], U32, align_bytes=64, name="codes_" + side, tag="codes_" + side)
+            scales[side] = keep.tile([P, PASSES, D], U8, align_bytes=64, name="scales_" + side, tag="scales_" + side)
+        held = keep.tile([P, TILES, T], F32, name="held", tag="held")
+        gains = []
+        for h in range(2):
+            gain = keep.tile([P, TILES, T], F32, name="gain%d" % h, tag="gain%d" % h)
+            gains.append(gain)
+
+        pieces = []
+
+        def add(src, c, side, n, c0, width, fmt):
+            pieces.append((src[c * ROWS : (c + 1) * ROWS, c0 : c0 + width], side, n, c0, width, fmt))
+
+        order = [["e",0],["v",0],["e",1],["v",1],["dy",0],["w",0],["dy",1],["w",1],["dy",2],["w",2],["dy",3],["w",3]]
+        halved = [3,4,5]
+        late = []
+        for name, c in order:
+            if name == "e":
+                add(e, c, "mov", c, 0, T, E4M3)
+            elif name == "dy":
+                add(dy, c, "mov", 2 + c, 0, T, E5M2)
+            else:
+                src = w if name == "w" else v
+                n = 2 + c if name == "w" else c
+                if n in halved:
+                    add(src, c, "stat", n, 0, HALF, E4M3)
+                    late.append((src, c, "stat", n, HALF, HALF, E4M3))
+                else:
+                    add(src, c, "stat", n, 0, D, E4M3)
+        first_late = len(pieces)
+        for a in late:
+            add(*a)
+
+        raw_tiles = []
+
+        def load(i):
+            src, side, n, c0, width, fmt = pieces[i]
+            raw = raws.tile([P, PACK, width], F32, name="raw", tag="raw")
+            nc.sync.dma_start(out=raw[:], in_=src.rearrange("(p j) c -> p j c", j=PACK))
+            raw_tiles.append(raw)
+
+        def copy_cols(eng, grouped, raw, c0, c1):
+            eng(
+                out=grouped[:, c0:c1, :].rearrange("p (c i) j -> p c j i", i=4),
+                in_=raw[:, :, c0:c1].rearrange("p j (c i) -> p c j i", i=4),
+            )
+
+        def copy_perm(eng, grouped, raw, h, m0, m1):
+            hs = slice(h * HALF, (h + 1) * HALF)
+            eng(
+                out=grouped[:, hs, :].rearrange("p (b m) j -> p m b j", b=TILES)[:, m0:m1],
+                in_=raw[:, :, hs].rearrange("p j (m b) -> p m b j", b=TILES)[:, m0:m1],
+            )
+
+        def cast(i, vcols):
+            src, side, n, c0, width, fmt = pieces[i]
+            raw = raw_tiles[i]
+            grouped = groups.tile([P, width, PACK], BF16, align_bytes=64, name="grouped", tag="grouped")
+            if PERM and side == "stat":
+                if width == D:
+                    m = (vcols - HALF) // TILES
+                    copy_perm(nc.vector.tensor_copy, grouped, raw, 0, 0, P)
+                    copy_perm(nc.scalar.copy, grouped, raw, 1, m, P)
+                    copy_perm(nc.vector.tensor_copy, grouped, raw, 1, 0, m)
+                else:
+                    m = vcols // TILES
+                    copy_perm(nc.vector.tensor_copy, grouped, raw, 0, 0, m)
+                    if m < P:
+                        copy_perm(nc.scalar.copy, grouped, raw, 0, m, P)
+            else:
+                copy_cols(nc.vector.tensor_copy, grouped, raw, 0, vcols)
+                if vcols < width:
+                    copy_cols(nc.scalar.copy, grouped, raw, vcols, width)
+            return grouped
+
+        def quantize(i, grouped, q0, q1):
+            src, side, n, c0, width, fmt = pieces[i]
+            nc.vector.quantize_mx(
+                out=codes[side][:, n, c0 + q0 : c0 + q1].bitcast(fmt),
+                scales=scales[side][:, n, c0 + q0 : c0 + q1],
+                in_=grouped[:, q0:q1, :].rearrange("p c j -> p (c j)"),
+            )
+
+        acc = {}
+
+        def multiply(n, b, t, start, stop):
+            d = slice(b * P, (b + 1) * P)
+            ts = slice(t * HALF, (t + 1) * HALF)
+            nc.tensor.matmul_mx(
+                out=acc[b, t][:],
+                lhsT=codes["stat"][:, n, d].bitcast(E4M3),
+                lhsT_scale=scales["stat"][:, n, d],
+                rhs=codes["mov"][:, n, ts].bitcast(E4M3 if n < 2 else E5M2),
+                rhs_scale=scales["mov"][:, n, ts],
+                start=start,
+                stop=stop,
+            )
+
+        def open_bank(b, t):
+            bank = psum.tile([P, HALF], F32, name="acc", tag="acc%d%d" % (b % TILES, t))
+            acc[b, t] = bank
+
+        def rows(x, h):
+            half = x[h * HALF : (h + 1) * HALF, :]
+            if PERM:
+                return half.rearrange("(p b) t -> p b t", b=TILES)
+            return half.rearrange("(b p) t -> p b t", p=P)
+
+        for b in range(TILES):
+            for t in range(2):
+                open_bank(b, t)
+
+        for i in range(RAW_BUFS):
+            load(i)
+
+        have = []
+        done = []
+        total = len(pieces)
+        for i in range(total):
+            src, side, n, c0, width, fmt = pieces[i]
+            if i >= first_late:
+                vcols = 512
+            else:
+                vcols = V_COLS if width == D else 320
+            grouped = cast(i, vcols)
+            if i + RAW_BUFS < total:
+                load(i + RAW_BUFS)
+            if i + RAW_BUFS == total - 1:
+                for h in range(2):
+                    for bb in range(0, TILES, 2):
+                        nc.sync.dma_start(out=gains[h][:, bb : bb + 2, :], in_=rows(g, h)[:, bb : bb + 2, :])
+            step = 1024 if width == D else 256
+            for q in range(0, width, step):
+                quantize(i, grouped, q, q + step)
+            if c0 == 0:
+                have.append((side, n))
+                if ("stat", n) in have and ("mov", n) in have:
+                    for b in range(TILES):
+                        for t in range(2):
+                            multiply(n, b, t, len(done) == 0, len(done) == PASSES - 1)
+                            if len(done) == PASSES - 1:
+                                nc.scalar.copy(out=held[:, b, t * HALF : (t + 1) * HALF], in_=acc[b, t][:])
+                    done.append(n)
+
+        for b in range(TILES):
+            nc.vector.tensor_mul(out=held[:, b, :], in0=held[:, b, :], in1=gains[0][:, b, :])
+            if not PERM:
+                nc.sync.dma_start(out=rows(out, 0)[:, b, :], in_=held[:, b, :])
+            elif b % 2 == 1:
+                nc.sync.dma_start(out=rows(out, 0)[:, b - 1 : b + 1, :], in_=held[:, b - 1 : b + 1, :])
+
+        early = [n for n in done if n not in halved]
+        tail = [n for n in done if n in halved]
+        for b in range(TILES, 2 * TILES):
+            for t in range(2):
+                open_bank(b, t)
+                for s, n in enumerate(early):
+                    multiply(n, b, t, s == 0, False)
+        for b in range(TILES, 2 * TILES):
+            for t in range(2):
+                for s, n in enumerate(tail):
+                    multiply(n, b, t, False, s == len(tail) - 1)
+                ts = slice(t * HALF, (t + 1) * HALF)
+                res = gains[1][:, b - TILES, ts]
+                nc.vector.tensor_mul(out=res, in0=acc[b, t][:], in1=res)
+                if b == 2 * TILES - 1:
+                    nc.sync.dma_start(out=rows(out, 1)[:, b - TILES, ts], in_=res)
+            if b < 2 * TILES - 1:
+                nc.sync.dma_start(out=rows(out, 1)[:, b - TILES, :], in_=gains[1][:, b - TILES, :])

@@ -49,7 +49,7 @@ def tile_mix_aux_fm_mul_kernel(tc, w, dy, v, e, g, out):
             pieces.append((src[c * ROWS : (c + 1) * ROWS, c0 : c0 + width], side, n, c0, width, fmt))
 
         order = [["e",0],["v",0],["e",1],["v",1],["dy",0],["w",0],["dy",1],["w",1],["dy",2],["w",2],["dy",3],["w",3]]
-        halved = [3,4,5]
+        halved = [4,5]
         late = []
         for name, c in order:
             if name == "e":
@@ -89,6 +89,12 @@ def tile_mix_aux_fm_mul_kernel(tc, w, dy, v, e, g, out):
                 in_=raw[:, :, hs].rearrange("p j (m b) -> p m b j", b=TILES)[:, m0:m1],
             )
 
+        def copy_part(eng, grouped, raw, b0, m0, m1):
+            eng(
+                out=grouped[:].rearrange("p (b m) j -> p m b j", b=TILES)[:, m0:m1, b0 : b0 + 2],
+                in_=raw[:].rearrange("p j (m b) -> p m b j", b=TILES)[:, m0:m1, b0 : b0 + 2],
+            )
+
         def cast(i, vcols):
             src, side, n, c0, width, fmt = pieces[i]
             raw = raw_tiles[i]
@@ -100,10 +106,12 @@ def tile_mix_aux_fm_mul_kernel(tc, w, dy, v, e, g, out):
                     copy_perm(nc.scalar.copy, grouped, raw, 1, m, P)
                     copy_perm(nc.vector.tensor_copy, grouped, raw, 1, 0, m)
                 else:
-                    m = vcols // TILES
-                    copy_perm(nc.vector.tensor_copy, grouped, raw, 0, 0, m)
-                    if m < P:
-                        copy_perm(nc.scalar.copy, grouped, raw, 0, m, P)
+                    for b0 in (0, 2):
+                        m = vcols // TILES
+                        copy_part(nc.vector.tensor_copy, grouped, raw, b0, 0, m)
+                        if m < P:
+                            copy_part(nc.scalar.copy, grouped, raw, b0, m, P)
+                        quantize(i, grouped, b0 * P, (b0 + 2) * P)
             else:
                 copy_cols(nc.vector.tensor_copy, grouped, raw, 0, vcols)
                 if vcols < width:
@@ -164,11 +172,11 @@ def tile_mix_aux_fm_mul_kernel(tc, w, dy, v, e, g, out):
                 load(i + RAW_BUFS)
             if i + RAW_BUFS == total - 1:
                 for h in range(2):
-                    for bb in range(0, TILES, 2):
-                        nc.sync.dma_start(out=gains[h][:, bb : bb + 2, :], in_=rows(g, h)[:, bb : bb + 2, :])
+                    nc.sync.dma_start(out=gains[h][:], in_=rows(g, h))
             step = 1024 if width == D else 256
-            for q in range(0, width, step):
-                quantize(i, grouped, q, q + step)
+            if width == D:
+                for q in range(0, width, step):
+                    quantize(i, grouped, q, q + step)
             if c0 == 0:
                 have.append((side, n))
                 if ("stat", n) in have and ("mov", n) in have:
@@ -202,5 +210,7 @@ def tile_mix_aux_fm_mul_kernel(tc, w, dy, v, e, g, out):
                 nc.vector.tensor_mul(out=res, in0=acc[b, t][:], in1=res)
                 if b == 2 * TILES - 1:
                     nc.sync.dma_start(out=rows(out, 1)[:, b - TILES, ts], in_=res)
-            if b < 2 * TILES - 1:
-                nc.sync.dma_start(out=rows(out, 1)[:, b - TILES, :], in_=gains[1][:, b - TILES, :])
+            if b == TILES + 1:
+                nc.sync.dma_start(out=rows(out, 1)[:, 0:2, :], in_=gains[1][:, 0:2, :])
+            if b == TILES + 2:
+                nc.sync.dma_start(out=rows(out, 1)[:, 2, :], in_=gains[1][:, 2, :])

@@ -18,9 +18,10 @@ ROWS = P * PACK
 HALF = 512
 TILES = HALF // P
 PASSES = (K + L) // ROWS
-PERM = True
+W_PASS = L // ROWS
 RAW_BUFS = 5
-V_COLS = 640
+VECTOR_COLS = 640
+FIRST_PASSES = 3
 
 
 def tile_mix_aux_fm_mul_kernel(tc, w, dy, v, e, g, out):
@@ -32,111 +33,99 @@ def tile_mix_aux_fm_mul_kernel(tc, w, dy, v, e, g, out):
         psum = ctx.enter_context(tc.psum_pool(name="psum", bufs=1))
         ctx.enter_context(tc.manual_schedule())
 
-        codes = {}
-        scales = {}
-        for side in ("stat", "mov"):
-            codes[side] = keep.tile([P, PASSES, D], U32, align_bytes=64, name="codes_" + side, tag="codes_" + side)
-            scales[side] = keep.tile([P, PASSES, D], U8, align_bytes=64, name="scales_" + side, tag="scales_" + side)
-        held = keep.tile([P, TILES, T], F32, name="held", tag="held")
-        gains = []
-        for h in range(2):
-            gain = keep.tile([P, TILES, T], F32, name="gain%d" % h, tag="gain%d" % h)
-            gains.append(gain)
+        stat_codes = keep.tile([P, PASSES, D], U32, align_bytes=64)
+        stat_scales = keep.tile([P, PASSES, D], U8, align_bytes=64)
+        mov_codes = keep.tile([P, PASSES, T], U32, align_bytes=64)
+        mov_scales = keep.tile([P, PASSES, T], U8, align_bytes=64)
+        held = keep.tile([P, TILES, T], F32)
+        gain0 = keep.tile([P, TILES, T], F32)
+        gain1 = keep.tile([P, TILES, T], F32)
 
-        pieces = []
-
-        def add(src, c, side, n, c0, width, fmt):
-            pieces.append((src[c * ROWS : (c + 1) * ROWS, c0 : c0 + width], side, n, c0, width, fmt))
-
-        order = [["e",0],["v",0],["e",1],["v",1],["dy",0],["w",0],["dy",1],["w",1],["dy",2],["w",2],["dy",3],["w",3]]
+        order = [["e",0],["v",0],["e",1],["v",1],["dy",0],["w",0],["dy",1],["w",1],["dy",2],["dy",3],["w",2],["w",3]]
         halved = [4,5]
-        late = []
+        source = {"w": w, "dy": dy, "v": v, "e": e}
+        pieces = []
         for name, c in order:
-            if name == "e":
-                add(e, c, "mov", c, 0, T, E4M3)
-            elif name == "dy":
-                add(dy, c, "mov", 2 + c, 0, T, E5M2)
-            else:
-                src = w if name == "w" else v
-                n = 2 + c if name == "w" else c
-                if n in halved:
-                    add(src, c, "stat", n, 0, HALF, E4M3)
-                    late.append((src, c, "stat", n, HALF, HALF, E4M3))
-                else:
-                    add(src, c, "stat", n, 0, D, E4M3)
+            n = c + (W_PASS if name in ("w", "dy") else 0)
+            width = HALF if name in ("w", "v") and n in halved else D
+            pieces.append((name, c, n, 0, width))
         first_late = len(pieces)
-        for a in late:
-            add(*a)
+        for name, c, n, c0, width in list(pieces):
+            if width == HALF:
+                pieces.append((name, c, n, HALF, HALF))
+
+        def d_rows(x, half):
+            return x[half * HALF : (half + 1) * HALF, :].rearrange("(p b) t -> p b t", b=TILES)
 
         raw_tiles = []
 
         def load(i):
-            src, side, n, c0, width, fmt = pieces[i]
-            raw = raws.tile([P, PACK, width], F32, name="raw", tag="raw")
-            nc.sync.dma_start(out=raw[:], in_=src.rearrange("(p j) c -> p j c", j=PACK))
+            if i == first_late:
+                nc.sync.dma_start(out=gain0[:], in_=d_rows(g, 0))
+            name, c, n, c0, width = pieces[i]
+            raw = raws.tile([P, PACK, width], F32)
+            rows = source[name][c * ROWS : (c + 1) * ROWS, c0 : c0 + width]
+            nc.sync.dma_start(out=raw[:], in_=rows.rearrange("(p j) c -> p j c", j=PACK))
             raw_tiles.append(raw)
+            if i == len(pieces) - 1:
+                nc.sync.dma_start(out=gain1[:], in_=d_rows(g, 1))
 
-        def copy_cols(eng, grouped, raw, c0, c1):
+        def copy_moving(eng, grouped, raw, c0, c1):
             eng(
                 out=grouped[:, c0:c1, :].rearrange("p (c i) j -> p c j i", i=4),
                 in_=raw[:, :, c0:c1].rearrange("p j (c i) -> p c j i", i=4),
             )
 
-        def copy_perm(eng, grouped, raw, h, m0, m1):
-            hs = slice(h * HALF, (h + 1) * HALF)
+        def copy_stationary(eng, grouped, raw, half, m0, m1, b0, b1):
+            cols = slice(half * HALF, (half + 1) * HALF)
             eng(
-                out=grouped[:, hs, :].rearrange("p (b m) j -> p m b j", b=TILES)[:, m0:m1],
-                in_=raw[:, :, hs].rearrange("p j (m b) -> p m b j", b=TILES)[:, m0:m1],
+                out=grouped[:, cols, :].rearrange("p (b m) j -> p m b j", b=TILES)[:, m0:m1, b0:b1],
+                in_=raw[:, :, cols].rearrange("p j (m b) -> p m b j", b=TILES)[:, m0:m1, b0:b1],
             )
-
-        def copy_part(eng, grouped, raw, b0, m0, m1):
-            eng(
-                out=grouped[:].rearrange("p (b m) j -> p m b j", b=TILES)[:, m0:m1, b0 : b0 + 2],
-                in_=raw[:].rearrange("p j (m b) -> p m b j", b=TILES)[:, m0:m1, b0 : b0 + 2],
-            )
-
-        def cast(i, vcols):
-            src, side, n, c0, width, fmt = pieces[i]
-            raw = raw_tiles[i]
-            grouped = groups.tile([P, width, PACK], BF16, align_bytes=64, name="grouped", tag="grouped")
-            if PERM and side == "stat":
-                if width == D:
-                    m = (vcols - HALF) // TILES
-                    copy_perm(nc.vector.tensor_copy, grouped, raw, 0, 0, P)
-                    copy_perm(nc.scalar.copy, grouped, raw, 1, m, P)
-                    copy_perm(nc.vector.tensor_copy, grouped, raw, 1, 0, m)
-                else:
-                    for b0 in (0, 2):
-                        m = vcols // TILES
-                        copy_part(nc.vector.tensor_copy, grouped, raw, b0, 0, m)
-                        if m < P:
-                            copy_part(nc.scalar.copy, grouped, raw, b0, m, P)
-                        quantize(i, grouped, b0 * P, (b0 + 2) * P)
-            else:
-                copy_cols(nc.vector.tensor_copy, grouped, raw, 0, vcols)
-                if vcols < width:
-                    copy_cols(nc.scalar.copy, grouped, raw, vcols, width)
-            return grouped
 
         def quantize(i, grouped, q0, q1):
-            src, side, n, c0, width, fmt = pieces[i]
+            name, c, n, c0, width = pieces[i]
+            moving = name in ("dy", "e")
+            codes = mov_codes if moving else stat_codes
+            scales = mov_scales if moving else stat_scales
             nc.vector.quantize_mx(
-                out=codes[side][:, n, c0 + q0 : c0 + q1].bitcast(fmt),
-                scales=scales[side][:, n, c0 + q0 : c0 + q1],
+                out=codes[:, n, c0 + q0 : c0 + q1].bitcast(E5M2 if name == "dy" else E4M3),
+                scales=scales[:, n, c0 + q0 : c0 + q1],
                 in_=grouped[:, q0:q1, :].rearrange("p c j -> p (c j)"),
             )
+
+        def prepare(i):
+            name, c, n, c0, width = pieces[i]
+            raw = raw_tiles[i]
+            grouped = groups.tile([P, width, PACK], BF16, align_bytes=64)
+            if width == HALF:
+                m = 80
+                for b0 in (0, 2):
+                    copy_stationary(nc.vector.tensor_copy, grouped, raw, 0, 0, m, b0, b0 + 2)
+                    copy_stationary(nc.scalar.copy, grouped, raw, 0, m, P, b0, b0 + 2)
+                    quantize(i, grouped, b0 * P, (b0 + 2) * P)
+                return
+            if name in ("dy", "e"):
+                copy_moving(nc.vector.tensor_copy, grouped, raw, 0, VECTOR_COLS)
+                copy_moving(nc.scalar.copy, grouped, raw, VECTOR_COLS, T)
+            else:
+                m = (VECTOR_COLS - HALF) // TILES
+                copy_stationary(nc.vector.tensor_copy, grouped, raw, 0, 0, P, 0, TILES)
+                copy_stationary(nc.scalar.copy, grouped, raw, 1, m, P, 0, TILES)
+                copy_stationary(nc.vector.tensor_copy, grouped, raw, 1, 0, m, 0, TILES)
+            quantize(i, grouped, 0, D)
 
         acc = {}
 
         def multiply(n, b, t, start, stop):
-            d = slice(b * P, (b + 1) * P)
-            ts = slice(t * HALF, (t + 1) * HALF)
+            d_cols = slice(b * P, (b + 1) * P)
+            t_cols = slice(t * HALF, (t + 1) * HALF)
             nc.tensor.matmul_mx(
                 out=acc[b, t][:],
-                lhsT=codes["stat"][:, n, d].bitcast(E4M3),
-                lhsT_scale=scales["stat"][:, n, d],
-                rhs=codes["mov"][:, n, ts].bitcast(E4M3 if n < 2 else E5M2),
-                rhs_scale=scales["mov"][:, n, ts],
+                lhsT=stat_codes[:, n, d_cols].bitcast(E4M3),
+                lhsT_scale=stat_scales[:, n, d_cols],
+                rhs=mov_codes[:, n, t_cols].bitcast(E4M3 if n < W_PASS else E5M2),
+                rhs_scale=mov_scales[:, n, t_cols],
                 start=start,
                 stop=stop,
             )
@@ -145,72 +134,54 @@ def tile_mix_aux_fm_mul_kernel(tc, w, dy, v, e, g, out):
             bank = psum.tile([P, HALF], F32, name="acc", tag="acc%d%d" % (b % TILES, t))
             acc[b, t] = bank
 
-        def rows(x, h):
-            half = x[h * HALF : (h + 1) * HALF, :]
-            if PERM:
-                return half.rearrange("(p b) t -> p b t", b=TILES)
-            return half.rearrange("(b p) t -> p b t", p=P)
-
-        for b in range(TILES):
-            for t in range(2):
-                open_bank(b, t)
-
         for i in range(RAW_BUFS):
             load(i)
 
-        have = []
+        ready = []
         done = []
-        total = len(pieces)
-        for i in range(total):
-            src, side, n, c0, width, fmt = pieces[i]
-            if i >= first_late:
-                vcols = 512
-            else:
-                vcols = V_COLS if width == D else 320
-            grouped = cast(i, vcols)
-            if i + RAW_BUFS < total:
+        for i in range(first_late):
+            prepare(i)
+            if i + RAW_BUFS < len(pieces):
                 load(i + RAW_BUFS)
-            if i + RAW_BUFS == total - 1:
-                for h in range(2):
-                    nc.sync.dma_start(out=gains[h][:], in_=rows(g, h))
-            step = 1024 if width == D else 256
-            if width == D:
-                for q in range(0, width, step):
-                    quantize(i, grouped, q, q + step)
-            if c0 == 0:
-                have.append((side, n))
-                if ("stat", n) in have and ("mov", n) in have:
-                    for b in range(TILES):
-                        for t in range(2):
-                            multiply(n, b, t, len(done) == 0, len(done) == PASSES - 1)
-                            if len(done) == PASSES - 1:
-                                nc.scalar.copy(out=held[:, b, t * HALF : (t + 1) * HALF], in_=acc[b, t][:])
-                    done.append(n)
+            name, c, n, c0, width = pieces[i]
+            if n not in ready:
+                ready.append(n)
+                continue
+            for b in range(TILES):
+                for t in range(2):
+                    if len(done) == 0:
+                        open_bank(b, t)
+                    multiply(n, b, t, len(done) == 0, len(done) == PASSES - 1)
+                    if len(done) == PASSES - 1:
+                        nc.scalar.copy(out=held[:, b, t * HALF : (t + 1) * HALF], in_=acc[b, t][:])
+            done.append(n)
 
-        for b in range(TILES):
-            nc.vector.tensor_mul(out=held[:, b, :], in0=held[:, b, :], in1=gains[0][:, b, :])
-            if not PERM:
-                nc.sync.dma_start(out=rows(out, 0)[:, b, :], in_=held[:, b, :])
-            elif b % 2 == 1:
-                nc.sync.dma_start(out=rows(out, 0)[:, b - 1 : b + 1, :], in_=held[:, b - 1 : b + 1, :])
+        def finish(b):
+            nc.vector.tensor_mul(out=held[:, b, :], in0=held[:, b, :], in1=gain0[:, b, :])
+            if b % 2 == 1:
+                nc.sync.dma_start(out=d_rows(out, 0)[:, b - 1 : b + 1, :], in_=held[:, b - 1 : b + 1, :])
 
-        early = [n for n in done if n not in halved]
-        tail = [n for n in done if n in halved]
+        finish(0)
+        finish(1)
+        prepare(first_late)
+        finish(2)
+        for i in range(first_late + 1, len(pieces)):
+            prepare(i)
+        finish(3)
+
         for b in range(TILES, 2 * TILES):
             for t in range(2):
                 open_bank(b, t)
-                for s, n in enumerate(early):
-                    multiply(n, b, t, s == 0, False)
+                for s in range(FIRST_PASSES):
+                    multiply(done[s], b, t, s == 0, False)
         for b in range(TILES, 2 * TILES):
+            q = b - TILES
             for t in range(2):
-                for s, n in enumerate(tail):
-                    multiply(n, b, t, False, s == len(tail) - 1)
-                ts = slice(t * HALF, (t + 1) * HALF)
-                res = gains[1][:, b - TILES, ts]
-                nc.vector.tensor_mul(out=res, in0=acc[b, t][:], in1=res)
-                if b == 2 * TILES - 1:
-                    nc.sync.dma_start(out=rows(out, 1)[:, b - TILES, ts], in_=res)
-            if b == TILES + 1:
-                nc.sync.dma_start(out=rows(out, 1)[:, 0:2, :], in_=gains[1][:, 0:2, :])
-            if b == TILES + 2:
-                nc.sync.dma_start(out=rows(out, 1)[:, 2, :], in_=gains[1][:, 2, :])
+                for s in range(FIRST_PASSES, PASSES):
+                    multiply(done[s], b, t, False, s == PASSES - 1)
+                t_cols = slice(t * HALF, (t + 1) * HALF)
+                nc.vector.tensor_mul(out=gain1[:, q, t_cols], in0=acc[b, t][:], in1=gain1[:, q, t_cols])
+                if q == TILES - 1:
+                    nc.sync.dma_start(out=d_rows(out, 1)[:, q, t_cols], in_=gain1[:, q, t_cols])
+            if q < TILES - 1:
+                nc.sync.dma_start(out=d_rows(out, 1)[:, q, :], in_=gain1[:, q, :])

@@ -19,7 +19,8 @@ HALF = 512
 TILES = HALF // P
 PASSES = (K + L) // ROWS
 W_PASS = L // ROWS
-RAW_BUFS = 5
+RAW_BUFS = 6
+AHEAD = 5
 VECTOR_COLS = 640
 FIRST_PASSES = 3
 
@@ -41,7 +42,7 @@ def tile_mix_aux_fm_mul_kernel(tc, w, dy, v, e, g, out):
         gain0 = keep.tile([P, TILES, T], F32)
         gain1 = keep.tile([P, TILES, T], F32)
 
-        order = [["e",0],["v",0],["e",1],["v",1],["dy",0],["w",0],["dy",1],["w",1],["dy",2],["dy",3],["w",2],["w",3]]
+        order = [["e",0],["v",0],["e",1],["v",1],["dy",0],["w",0],["dy",1],["dy",2],["w",1],["dy",3],["w",2],["w",3]]
         halved = [4,5]
         source = {"w": w, "dy": dy, "v": v, "e": e}
         pieces = []
@@ -65,7 +66,8 @@ def tile_mix_aux_fm_mul_kernel(tc, w, dy, v, e, g, out):
             name, c, n, c0, width = pieces[i]
             raw = raws.tile([P, PACK, width], F32)
             rows = source[name][c * ROWS : (c + 1) * ROWS, c0 : c0 + width]
-            nc.sync.dma_start(out=raw[:], in_=rows.rearrange("(p j) c -> p j c", j=PACK))
+            queue = nc.scalar if i % 2 == 1 and width == D else nc.sync
+            queue.dma_start(out=raw[:], in_=rows.rearrange("(p j) c -> p j c", j=PACK))
             raw_tiles.append(raw)
             if i == len(pieces) - 1:
                 nc.sync.dma_start(out=gain1[:], in_=d_rows(g, 1))
@@ -134,15 +136,15 @@ def tile_mix_aux_fm_mul_kernel(tc, w, dy, v, e, g, out):
             bank = psum.tile([P, HALF], F32, name="acc", tag="acc%d%d" % (b % TILES, t))
             acc[b, t] = bank
 
-        for i in range(RAW_BUFS):
+        for i in range(AHEAD):
             load(i)
 
         ready = []
         done = []
         for i in range(first_late):
             prepare(i)
-            if i + RAW_BUFS < len(pieces):
-                load(i + RAW_BUFS)
+            if i + AHEAD < len(pieces):
+                load(i + AHEAD)
             name, c, n, c0, width = pieces[i]
             if n not in ready:
                 ready.append(n)
@@ -159,7 +161,8 @@ def tile_mix_aux_fm_mul_kernel(tc, w, dy, v, e, g, out):
         def finish(b):
             nc.vector.tensor_mul(out=held[:, b, :], in0=held[:, b, :], in1=gain0[:, b, :])
             if b % 2 == 1:
-                nc.sync.dma_start(out=d_rows(out, 0)[:, b - 1 : b + 1, :], in_=held[:, b - 1 : b + 1, :])
+                queue = nc.sync if b == 1 else nc.scalar
+                queue.dma_start(out=d_rows(out, 0)[:, b - 1 : b + 1, :], in_=held[:, b - 1 : b + 1, :])
 
         finish(0)
         finish(1)
@@ -182,6 +185,8 @@ def tile_mix_aux_fm_mul_kernel(tc, w, dy, v, e, g, out):
                 t_cols = slice(t * HALF, (t + 1) * HALF)
                 nc.vector.tensor_mul(out=gain1[:, q, t_cols], in0=acc[b, t][:], in1=gain1[:, q, t_cols])
                 if q == TILES - 1:
-                    nc.sync.dma_start(out=d_rows(out, 1)[:, q, t_cols], in_=gain1[:, q, t_cols])
+                    queue = nc.scalar if t == 0 else nc.sync
+                    queue.dma_start(out=d_rows(out, 1)[:, q, t_cols], in_=gain1[:, q, t_cols])
             if q < TILES - 1:
-                nc.sync.dma_start(out=d_rows(out, 1)[:, q, :], in_=gain1[:, q, :])
+                queue = nc.scalar if q == 1 else nc.sync
+                queue.dma_start(out=d_rows(out, 1)[:, q, :], in_=gain1[:, q, :])

@@ -19,9 +19,8 @@ HALF = 512
 TILES = HALF // P
 PASSES = (K + L) // ROWS
 W_PASS = L // ROWS
-RAW_BUFS = 6
-AHEAD = 5
-VECTOR_COLS = 640
+RAW_BUFS = 5
+VECTOR_COLS = 704
 FIRST_PASSES = 3
 
 
@@ -66,8 +65,7 @@ def tile_mix_aux_fm_mul_kernel(tc, w, dy, v, e, g, out):
             name, c, n, c0, width = pieces[i]
             raw = raws.tile([P, PACK, width], F32)
             rows = source[name][c * ROWS : (c + 1) * ROWS, c0 : c0 + width]
-            queue = nc.scalar if i % 2 == 1 and width == D else nc.sync
-            queue.dma_start(out=raw[:], in_=rows.rearrange("(p j) c -> p j c", j=PACK))
+            nc.sync.dma_start(out=raw[:], in_=rows.rearrange("(p j) c -> p j c", j=PACK))
             raw_tiles.append(raw)
             if i == len(pieces) - 1:
                 nc.sync.dma_start(out=gain1[:], in_=d_rows(g, 1))
@@ -101,7 +99,7 @@ def tile_mix_aux_fm_mul_kernel(tc, w, dy, v, e, g, out):
             raw = raw_tiles[i]
             grouped = groups.tile([P, width, PACK], BF16, align_bytes=64)
             if width == HALF:
-                m = 80
+                m = 88
                 for b0 in (0, 2):
                     copy_stationary(nc.vector.tensor_copy, grouped, raw, 0, 0, m, b0, b0 + 2)
                     copy_stationary(nc.scalar.copy, grouped, raw, 0, m, P, b0, b0 + 2)
@@ -136,15 +134,15 @@ def tile_mix_aux_fm_mul_kernel(tc, w, dy, v, e, g, out):
             bank = psum.tile([P, HALF], F32, name="acc", tag="acc%d%d" % (b % TILES, t))
             acc[b, t] = bank
 
-        for i in range(AHEAD):
+        for i in range(RAW_BUFS):
             load(i)
 
         ready = []
         done = []
         for i in range(first_late):
             prepare(i)
-            if i + AHEAD < len(pieces):
-                load(i + AHEAD)
+            if i + RAW_BUFS < len(pieces):
+                load(i + RAW_BUFS)
             name, c, n, c0, width = pieces[i]
             if n not in ready:
                 ready.append(n)
@@ -161,8 +159,7 @@ def tile_mix_aux_fm_mul_kernel(tc, w, dy, v, e, g, out):
         def finish(b):
             nc.vector.tensor_mul(out=held[:, b, :], in0=held[:, b, :], in1=gain0[:, b, :])
             if b % 2 == 1:
-                queue = nc.sync if b == 1 else nc.scalar
-                queue.dma_start(out=d_rows(out, 0)[:, b - 1 : b + 1, :], in_=held[:, b - 1 : b + 1, :])
+                nc.sync.dma_start(out=d_rows(out, 0)[:, b - 1 : b + 1, :], in_=held[:, b - 1 : b + 1, :])
 
         finish(0)
         finish(1)
@@ -185,8 +182,6 @@ def tile_mix_aux_fm_mul_kernel(tc, w, dy, v, e, g, out):
                 t_cols = slice(t * HALF, (t + 1) * HALF)
                 nc.vector.tensor_mul(out=gain1[:, q, t_cols], in0=acc[b, t][:], in1=gain1[:, q, t_cols])
                 if q == TILES - 1:
-                    queue = nc.scalar if t == 0 else nc.sync
-                    queue.dma_start(out=d_rows(out, 1)[:, q, t_cols], in_=gain1[:, q, t_cols])
+                    nc.sync.dma_start(out=d_rows(out, 1)[:, q, t_cols], in_=gain1[:, q, t_cols])
             if q < TILES - 1:
-                queue = nc.scalar if q == 1 else nc.sync
-                queue.dma_start(out=d_rows(out, 1)[:, q, :], in_=gain1[:, q, :])
+                nc.sync.dma_start(out=d_rows(out, 1)[:, q, :], in_=gain1[:, q, :])

from contextlib import ExitStack

import concourse.mybir as mybir

K, L, D, T = 2048, 1024, 1024, 1024
FLOPS = 2 * D * T * (K + L)

F32 = mybir.dt.float32
BF16 = mybir.dt.bfloat16
U32 = mybir.dt.uint32
U8 = mybir.dt.uint8
E4M3 = mybir.dt.float8_e4m3fn_x4
E5M2 = mybir.dt.float8_e5m2_x4

P = 128
PACK = 4
ROWS = P * PACK
HALF = 512
TILES = HALF // P
PASSES = (K + L) // ROWS
W_PASS = L // ROWS
RAW_BUFS = 5
VECTOR_COLS = 704
FIRST_PASSES = 3


def tile_mix_aux_fm_mul_kernel(tc, w, dy, v, e, g, out):
    nc = tc.nc
    with ExitStack() as ctx:
        raws = ctx.enter_context(tc.tile_pool(name="raws", bufs=RAW_BUFS))
        groups = ctx.enter_context(tc.tile_pool(name="groups", bufs=3))
        keep = ctx.enter_context(tc.tile_pool(name="keep", bufs=1))
        psum = ctx.enter_context(tc.psum_pool(name="psum", bufs=1))
        ctx.enter_context(tc.manual_schedule())

        stat_codes = keep.tile([P, PASSES, D], U32, align_bytes=64)
        stat_scales = keep.tile([P, PASSES, D], U8, align_bytes=64)
        mov_codes = keep.tile([P, PASSES, T], U32, align_bytes=64)
        mov_scales = keep.tile([P, PASSES, T], U8, align_bytes=64)
        held = keep.tile([P, TILES, T], F32)
        gain0 = keep.tile([P, TILES, T], F32)
        gain1 = keep.tile([P, TILES, T], F32)

        order = [["e",0],["v",0],["e",1],["v",1],["dy",0],["w",0],["dy",1],["dy",2],["w",1],["dy",3],["w",2],["w",3]]
        halved = [4,5]
        source = {"w": w, "dy": dy, "v": v, "e": e}
        pieces = []
        for name, c in order:
            n = c + (W_PASS if name in ("w", "dy") else 0)
            width = HALF if name in ("w", "v") and n in halved else D
            pieces.append((name, c, n, 0, width))
        first_late = len(pieces)
        for name, c, n, c0, width in list(pieces):
            if width == HALF:
                pieces.append((name, c, n, HALF, HALF))

        def d_rows(x, half):
            return x[half * HALF : (half + 1) * HALF, :].rearrange("(p b) t -> p b t", b=TILES)

        raw_tiles = []

        def load(i):
            if i == first_late:
                nc.sync.dma_start(out=gain0[:], in_=d_rows(g, 0))
            name, c, n, c0, width = pieces[i]
            raw = raws.tile([P, PACK, width], F32)
            rows = source[name][c * ROWS : (c + 1) * ROWS, c0 : c0 + width]
            nc.sync.dma_start(out=raw[:], in_=rows.rearrange("(p j) c -> p j c", j=PACK))
            raw_tiles.append(raw)
            if i == len(pieces) - 1:
                nc.sync.dma_start(out=gain1[:], in_=d_rows(g, 1))

        def copy_moving(eng, grouped, raw, c0, c1):
            eng(
                out=grouped[:, c0:c1, :].rearrange("p (c i) j -> p c j i", i=4),
                in_=raw[:, :, c0:c1].rearrange("p j (c i) -> p c j i", i=4),
            )

        def copy_stationary(eng, grouped, raw, half, m0, m1, b0, b1):
            cols = slice(half * HALF, (half + 1) * HALF)
            eng(
                out=grouped[:, cols, :].rearrange("p (b m) j -> p m b j", b=TILES)[:, m0:m1, b0:b1],
                in_=raw[:, :, cols].rearrange("p j (m b) -> p m b j", b=TILES)[:, m0:m1, b0:b1],
            )

        def quantize(i, grouped, q0, q1):
            name, c, n, c0, width = pieces[i]
            moving = name in ("dy", "e")
            codes = mov_codes if moving else stat_codes
            scales = mov_scales if moving else stat_scales
            nc.vector.quantize_mx(
                out=codes[:, n, c0 + q0 : c0 + q1].bitcast(E5M2 if name == "dy" else E4M3),
                scales=scales[:, n, c0 + q0 : c0 + q1],
                in_=grouped[:, q0:q1, :].rearrange("p c j -> p (c j)"),
            )

        def prepare(i):
            name, c, n, c0, width = pieces[i]
            raw = raw_tiles[i]
            grouped = groups.tile([P, width, PACK], BF16, align_bytes=64)
            if width == HALF:
                m = 88
                for b0 in (0, 2):
                    copy_stationary(nc.vector.tensor_copy, grouped, raw, 0, 0, m, b0, b0 + 2)
                    copy_stationary(nc.scalar.copy, grouped, raw, 0, m, P, b0, b0 + 2)
                    quantize(i, grouped, b0 * P, (b0 + 2) * P)
                return
            if name in ("dy", "e"):
                copy_moving(nc.vector.tensor_copy, grouped, raw, 0, VECTOR_COLS)
                copy_moving(nc.scalar.copy, grouped, raw, VECTOR_COLS, T)
            else:
                m = (VECTOR_COLS - HALF) // TILES
                copy_stationary(nc.vector.tensor_copy, grouped, raw, 0, 0, P, 0, TILES)
                copy_stationary(nc.scalar.copy, grouped, raw, 1, m, P, 0, TILES)
                copy_stationary(nc.vector.tensor_copy, grouped, raw, 1, 0, m, 0, TILES)
            quantize(i, grouped, 0, D)

        acc = {}

        def multiply(n, b, t, start, stop):
            d_cols = slice(b * P, (b + 1) * P)
            t_cols = slice(t * HALF, (t + 1) * HALF)
            nc.tensor.matmul_mx(
                out=acc[b, t][:],
                lhsT=stat_codes[:, n, d_cols].bitcast(E4M3),
                lhsT_scale=stat_scales[:, n, d_cols],
                rhs=mov_codes[:, n, t_cols].bitcast(E4M3 if n < W_PASS else E5M2),
                rhs_scale=mov_scales[:, n, t_cols],
                start=start,
                stop=stop,
            )

        def open_bank(b, t):
            bank = psum.tile([P, HALF], F32, name="acc", tag="acc%d%d" % (b % TILES, t))
            acc[b, t] = bank

        for i in range(RAW_BUFS):
            load(i)

        ready = []
        done = []
        for i in range(first_late):
            prepare(i)
            if i + RAW_BUFS < len(pieces):
                load(i + RAW_BUFS)
            name, c, n, c0, width = pieces[i]
            if n not in ready:
                ready.append(n)
                continue
            for b in range(TILES):
                for t in range(2):
                    if len(done) == 0:
                        open_bank(b, t)
                    multiply(n, b, t, len(done) == 0, len(done) == PASSES - 1)
                    if len(done) == PASSES - 1:
                        nc.scalar.copy(out=held[:, b, t * HALF : (t + 1) * HALF], in_=acc[b, t][:])
            done.append(n)

        def finish(b):
            nc.vector.tensor_mul(out=held[:, b, :], in0=held[:, b, :], in1=gain0[:, b, :])
            if b % 2 == 1:
                nc.sync.dma_start(out=d_rows(out, 0)[:, b - 1 : b + 1, :], in_=held[:, b - 1 : b + 1, :])

        finish(0)
        finish(1)
        prepare(first_late)
        finish(2)
        for i in range(first_late + 1, len(pieces)):
            prepare(i)
        finish(3)

        for b in range(TILES, 2 * TILES):
            for t in range(2):
                open_bank(b, t)
                for s in range(FIRST_PASSES):
                    multiply(done[s], b, t, s == 0, False)
        for b in range(TILES, 2 * TILES):
            q = b - TILES
            for t in range(2):
                for s in range(FIRST_PASSES, PASSES):
                    multiply(done[s], b, t, False, s == PASSES - 1)
                t_cols = slice(t * HALF, (t + 1) * HALF)
                nc.vector.tensor_mul(out=gain1[:, q, t_cols], in0=acc[b, t][:], in1=gain1[:, q, t_cols])
                if q == TILES - 1:
                    nc.sync.dma_start(out=d_rows(out, 1)[:, q, t_cols], in_=gain1[:, q, t_cols])
            if q < TILES - 1:
                nc.sync.dma_start(out=d_rows(out, 1)[:, q, :], in_=gain1[:, q, :])
